import numpy as np
import ml_dtypes


def mxq(x, axis, fmt="e4m3"):
    dtype, down = {"e4m3": (ml_dtypes.float8_e4m3fn, 7), "e5m2": (ml_dtypes.float8_e5m2, 14)}[fmt]
    v = np.moveaxis(np.asarray(x, np.float32).astype(ml_dtypes.bfloat16).astype(np.float64), axis, -1)
    blocks = v.reshape(v.shape[:-1] + (-1, 32))
    amax = np.abs(blocks).max(-1, keepdims=True)
    byte = np.maximum(np.where(amax > 0, np.frexp(amax)[1] - 1 + 127, 0) - down, 1)
    scale = np.exp2(byte - 127.0)
    codes = (blocks / scale).astype(np.float32).astype(dtype).astype(np.float64)
    return np.moveaxis((codes * scale).reshape(v.shape), -1, axis)


WIDE = False


def mx_kscale(k):
    if not WIDE:
        return np.ones(k)
    levels = np.array([10, -10, 5, -5, 0])
    if k % 512:
        return np.exp2(np.random.permutation(np.resize(levels, k // 32))).repeat(32)
    a = np.empty((k // 512, 16))
    for p in range(k // 512):
        a[p, :8] = np.random.permutation(np.resize(levels, 8))
        for g in range(8):
            far = levels[np.abs(levels - a[p, g]) >= 10]
            a[p, g + 8] = far[np.random.randint(len(far))]
    return np.exp2(a.ravel()).repeat(32)


def f64(x):
    return np.asarray(x).astype(np.float64)


def striped(idx):
    return np.tile(np.asarray(idx).reshape(-1, 16).T, (8, 1)).astype(np.uint16)


def unstriped(offs):
    return offs[:16].T.reshape(-1).astype(np.int64)


E2M1 = np.array([0.0, 0.5, 1.0, 1.5, 2.0, 3.0, 4.0, 6.0, -0.0, -0.5, -1.0, -1.5, -2.0, -3.0, -4.0, -6.0])


def pack_weight(w, fmt):
    k, n = w.shape
    w = f64(np.asarray(w, np.float32).astype(ml_dtypes.bfloat16)).reshape(k // 32, 32, n)
    amax = np.abs(w).max(1)
    if fmt == "e4m3":
        byte = np.frexp(amax)[1] - 1 + 127 - 7
    else:
        mant, ex = np.frexp(amax / 6.0)
        byte = np.where(mant > 0.5, ex, ex - 1) + 127
    byte = np.clip(np.where(amax > 0, byte, 1), 1, 254)
    scaled = (w * np.exp2(127.0 - byte)[:, None, :]).reshape(k, n).astype(np.float32)
    by_word = np.ascontiguousarray(scaled.reshape(k // 512, 128, 4, n).transpose(0, 1, 3, 2))
    if fmt == "e4m3":
        words = by_word.astype(ml_dtypes.float8_e4m3fn).view(np.uint8)
    else:
        c = by_word.astype(ml_dtypes.float4_e2m1fn).view(np.uint8) & 0xF
        words = (c[..., 0::2] | (c[..., 1::2] << 4)).reshape(k // 512, 128, 2 * n)
    return np.ascontiguousarray(words), np.ascontiguousarray(byte.astype(np.uint8).reshape(k // 512, 16, n))


def unpack_weight(words, scales, fmt):
    g, _, n = scales.shape
    words = np.ascontiguousarray(words).reshape(g, 128, n, -1)
    if fmt == "e4m3":
        vals = words.view(ml_dtypes.float8_e4m3fn).astype(np.float64)
    else:
        nib = np.empty((g, 128, n, 4), np.uint8)
        nib[..., 0::2] = words & 0xF
        nib[..., 1::2] = words >> 4
        vals = E2M1[nib]
    vals = vals * np.repeat(np.exp2(scales.astype(np.float64) - 127.0), 8, axis=1)[..., None]
    return vals.transpose(0, 1, 3, 2).reshape(g * 512, n)


def silu(v):
    return v / (1.0 + np.exp(-v))


def bf(x):
    return np.asarray(x, np.float32).astype(ml_dtypes.bfloat16)


def planes(Y):
    r, m = Y.shape
    b = f64(bf(Y)).reshape(r // 32, 32, m)
    amax = np.abs(b).max(1)
    byte = np.clip(np.where(amax > 0, np.frexp(amax)[1] - 1 + 127 - 7, 1), 1, 254)
    codes = (b * np.exp2(127.0 - byte)[:, None, :]).reshape(r, m).astype(np.float32).astype(ml_dtypes.float8_e4m3fn).view(np.uint8)
    words = codes.reshape(r // 512, 128, 4, m).transpose(0, 1, 3, 2)
    return np.ascontiguousarray(words), np.ascontiguousarray(byte.astype(np.uint8).reshape(r // 512, 16, m))


K, T, U, V, J, L, N = 512, 1024, 1024, 1024, 512, 512, 512


def setup_inputs():
    n = np.random.standard_normal
    idx = np.random.permutation(T)[:J]
    idx2 = np.random.permutation(U)[:J]
    idx3 = np.random.permutation(V)[:J]
    fk = mx_kscale(K)
    fl = mx_kscale(L)
    wp = pack_weight(n((K, N)) * 1 / np.sqrt(K) * fk[:, None], "e4m3")
    dxp = pack_weight(n((L, J)) / fl[:, None], "e2m1")
    wdp = pack_weight(n((L, N)) * 1 / np.sqrt(L) * fl[:, None], "e4m3")
    return {
        "xa": (n((K, T))).astype(np.float32),
        "xb": (n((K, U))).astype(np.float32),
        "xc": (n((K, V))).astype(np.float32),
        "fk": (np.random.uniform(0.5, 2.0, (K, 1)) / fk[:, None]).astype(np.float32),
        "w_words": wp[0],
        "w_scales": wp[1],
        "dx_words": dxp[0],
        "dx_scales": dxp[1],
        "wd_words": wdp[0],
        "wd_scales": wdp[1],
        "offs": striped(idx),
        "offs2": striped(idx2),
        "offs3": striped(idx3),
    }


def reference(xa, xb, xc, fk, w_words, w_scales, dx_words, dx_scales, wd_words, wd_scales, offs, offs2, offs3):
    idx = unstriped(offs)
    idx2 = unstriped(offs2)
    idx3 = unstriped(offs3)
    wu = unpack_weight(w_words, w_scales, "e4m3")
    dxu = unpack_weight(dx_words, dx_scales, "e2m1")
    wdu = unpack_weight(wd_words, wd_scales, "e4m3")
    s = (f64(xa)[:, idx] + f64(xb)[:, idx2] + f64(xc)[:, idx3]) * f64(fk)
    sq = mxq(s, 0, "e4m3")
    z = wu.T @ sq + wdu.T @ dxu
    y = silu(0.6 * z)
    words, scales = planes(y)
    return y, words, scales

@@ -1,0 +1,185 @@
+from contextlib import ExitStack
+
+import concourse.mybir as mybir
+
+K, T, J, N = 512, 1024, 512, 512
+FLOPS = 2 * 2 * K * N * J
+
+F32 = mybir.dt.float32
+BF16 = mybir.dt.bfloat16
+I32 = mybir.dt.int32
+U16 = mybir.dt.uint16
+U8 = mybir.dt.uint8
+FP8X4 = mybir.dt.float8_e4m3fn_x4
+FP4X4 = mybir.dt.float4_e2m1fn_x4
+ADD = mybir.AluOpType.add
+COPY = mybir.ActivationFunctionType.Copy
+SILU = mybir.ActivationFunctionType.Silu
+
+P = 128
+PACK = 4
+PARTS = 4
+W = J // PARTS
+W_ROW = 4
+
+
+def tile_list_three_tables_summed_pl_kernel(
+    tc, xa, xb, xc, fk, w_words, w_scales, dx_words, dx_scales, wd_words, wd_scales,
+    offs, offs2, offs3, out_0, out_1, out_2,
+):
+    nc = tc.nc
+    with ExitStack() as ctx:
+        keep = ctx.enter_context(tc.tile_pool(name="keep", bufs=1))
+        ring = ctx.enter_context(tc.tile_pool(name="ring", bufs=2))
+        psum = ctx.enter_context(tc.psum_pool(name="psum", bufs=1))
+
+        lists = {}
+        for name in ("c", "a", "b"):
+            lists[name] = keep.tile([P, J // 16], U16, name="list_" + name)
+        list_src = {"a": offs, "b": offs2, "c": offs3}
+        table_src = {"a": xa, "b": xb, "c": xc}
+        planes = {}
+        for name in ("c", "a", "b"):
+            for t in range(PACK):
+                planes[name, t] = keep.tile([P, T], F32, name="plane_%s%d" % (name, t))
+
+        fk_sb = keep.tile([P, PACK], F32)
+        w_raw = keep.tile([P, N], I32)
+        wd_raw = keep.tile([P, N], I32)
+        w_dealt = keep.tile([P, N], I32, align_bytes=64)
+        wd_dealt = keep.tile([P, N], I32, align_bytes=64)
+        wscale_raw = keep.tile([P, N], U8)
+        wscale = keep.tile([P, N], U8, align_bytes=64)
+        dx_codes = keep.tile([P, 2 * J], U8, align_bytes=64)
+        dx_scale = keep.tile([P, J], U8, align_bytes=64)
+        warm = keep.tile([P, 2], F32)
+
+        nc.vector.memset(wscale_raw[:].bitcast(I32), 0)
+        nc.vector.memset(dx_scale[:].bitcast(I32), 0)
+        nc.vector.memset(warm[:, 0:1], 0.0)
+        nc.scalar.activation(warm[:, 1:2], warm[:, 0:1], SILU)
+
+        def load_plane(name, t):
+            rows = table_src[name].rearrange("(p t) u -> p t u", t=PACK)
+            nc.sync.dma_start(planes[name, t][:], rows[:, t, :])
+
+        def load_list(name):
+            nc.sync.dma_start(lists[name][:], list_src[name])
+
+        def load_scales(tile, src, row, q):
+            nc.sync.dma_start(
+                tile[32 * q + row : 32 * q + row + 4, :].bitcast(I32),
+                src[0][4 * q : 4 * q + 4, :].bitcast(I32),
+            )
+
+        def load_words(tile, src):
+            nc.sync.dma_start(tile[:], src[0].rearrange("p n t -> p (n t)").bitcast(I32))
+
+        order = [("c", 0), ("c", 1), ("a", 0), ("a", 1), ("b", 0), ("c", 2),
+                 ("b", 1), ("a", 2), ("c", 3), ("b", 2), ("a", 3), ("b", 3)]
+        small = [lambda: load_list("c"), lambda: load_list("a"), lambda: load_list("b"),
+                 lambda: nc.sync.dma_start(fk_sb[:], fk.rearrange("(p t) o -> p (t o)", t=PACK))]
+        for q in range(4):
+            small.append(lambda q=q: load_scales(wscale_raw, wd_scales, 0, q))
+        for q in range(4):
+            small.append(lambda q=q: load_scales(wscale_raw, w_scales, W_ROW, q))
+        for q in range(4):
+            small.append(lambda q=q: load_scales(dx_scale, dx_scales, 0, q))
+        large = [lambda name=name, t=t: load_plane(name, t) for name, t in order]
+        large.insert(6, lambda: load_words(wd_raw, wd_words))
+        large.insert(8, lambda: load_words(w_raw, w_words))
+        large.insert(10, lambda: nc.sync.dma_start(dx_codes[:].bitcast(I32), dx_words[0].bitcast(I32)))
+        for i in range(len(large)):
+            large[i]()
+            small[i]()
+            if i == 5:
+                small[15]()
+
+        s_bf = keep.tile([P, J, PACK], BF16, align_bytes=64)
+        partial = {}
+
+        def gather(name, t, cols, into):
+            picked = planes[name, t][:].indirect(lists[name][:, cols.start // 16 : cols.stop // 16])
+            if name == "c":
+                nc.vector.tensor_copy(into, picked)
+            else:
+                nc.vector.tensor_tensor(into, picked, partial[t, cols.start], ADD)
+
+        def scale_round(t, cols, src):
+            nc.scalar.activation(s_bf[:, cols, t], src, COPY, scale=fk_sb[:, t : t + 1])
+
+        whole = slice(0, J)
+        for name, t in order[:-2]:
+            dst = keep.tile([P, J], F32, name="sum_%s%d" % (name, t))
+            gather(name, t, whole, dst[:])
+            partial[t, 0] = dst[:]
+            if name == "b":
+                scale_round(t, whole, dst[:])
+            if (name, t) == ("b", 1):
+                nc.vector.tensor_copy(
+                    wd_dealt[:].rearrange("p (t m) -> p m t", t=PACK),
+                    wd_raw[:].rearrange("p (m t) -> p m t", t=PACK))
+            if (name, t) == ("a", 2):
+                nc.vector.tensor_copy(
+                    w_dealt[:].rearrange("p (t m) -> p m t", t=PACK),
+                    w_raw[:].rearrange("p (m t) -> p m t", t=PACK))
+            if (name, t) == ("b", 2):
+                nc.vector.tensor_copy(
+                    wscale[:].rearrange("p (t m) -> p t m", t=PACK),
+                    wscale_raw[:].rearrange("p (m t) -> p t m", t=PACK))
+
+        banks = [psum.tile([P, PACK, W], F32, name="bank%d" % q) for q in range(PARTS)]
+        for q in range(PARTS):
+            for t in range(PACK):
+                nc.tensor.matmul_mx(
+                    banks[q][:, t, :],
+                    lhsT=wd_dealt[:, t * P : (t + 1) * P].bitcast(FP8X4),
+                    lhsT_scale=wscale[:, t * P : (t + 1) * P],
+                    rhs=dx_codes[:, 2 * q * W : 2 * (q + 1) * W].bitcast(FP4X4),
+                    rhs_scale=dx_scale[:, q * W : (q + 1) * W],
+                    start=(t == 0), stop=False)
+
+        last = PACK - 1
+        c_last = partial[last, 0]
+        s_codes = keep.tile([P, J], I32, align_bytes=64)
+        s_scale = keep.tile([P, J], U8, align_bytes=64)
+        y_codes = keep.tile([P, J], I32, align_bytes=64)
+        y_scale = keep.tile([P, J], U8, align_bytes=64)
+        out_rows = out_0.rearrange("(p t) j -> p t j", t=PACK)
+        out_words = out_1[0].rearrange("p c r -> p (c r)").bitcast(I32)
+        for q in range(PARTS):
+            cols = slice(q * W, (q + 1) * W)
+            two = ring.tile([P, W], F32, name="two")
+            partial[last, cols.start] = c_last[:, cols]
+            gather("a", last, cols, two[:])
+            three = keep.tile([P, W], F32, name="three%d" % q)
+            partial[last, cols.start] = two[:]
+            gather("b", last, cols, three[:])
+            scale_round(last, cols, three[:])
+            nc.vector.quantize_mx(
+                s_codes[:, cols].bitcast(FP8X4), s_scale[:, cols],
+                s_bf[:, cols, :].rearrange("p j t -> p (j t)"))
+            for t in range(PACK):
+                nc.tensor.matmul_mx(
+                    banks[q][:, t, :],
+                    lhsT=w_dealt[:, t * P : (t + 1) * P].bitcast(FP8X4),
+                    lhsT_scale=wscale[W_ROW:, t * P : (t + 1) * P],
+                    rhs=s_codes[:, cols].bitcast(FP8X4),
+                    rhs_scale=s_scale[:, cols],
+                    start=False, stop=(t == last))
+            y = keep.tile([P, PACK, W], F32, name="y%d" % q)
+            nc.scalar.activation(y[:], banks[q][:], SILU, scale=0.6)
+            nc.sync.dma_start(out_rows[:, :, cols], y[:])
+            y_bf = keep.tile([P, W, PACK], BF16, name="y_bf%d" % q, align_bytes=64)
+            nc.vector.tensor_copy(
+                y_bf[:].rearrange("p (c i) t -> p c t i", i=4),
+                y[:].rearrange("p t (c i) -> p c t i", i=4))
+            nc.vector.quantize_mx(
+                y_codes[:, cols].bitcast(FP8X4), y_scale[:, cols],
+                y_bf[:].rearrange("p j t -> p (j t)"))
+            nc.sync.dma_start(out_words[:, cols], y_codes[:, cols])
+        for q in range(4):
+            eng = nc.scalar if q % 2 else nc.sync
+            eng.dma_start(
+                out_2[0][4 * q : 4 * q + 4, :].bitcast(I32),
+                y_scale[32 * q : 32 * q + 4, :].bitcast(I32))

@@ -30,7 +30,6 @@ def tile_list_three_tables_summed_pl_kernel(
     nc = tc.nc
     with ExitStack() as ctx:
         keep = ctx.enter_context(tc.tile_pool(name="keep", bufs=1))
-        ring = ctx.enter_context(tc.tile_pool(name="ring", bufs=2))
         psum = ctx.enter_context(tc.psum_pool(name="psum", bufs=1))
 
         lists = {}
@@ -49,7 +48,6 @@ def tile_list_three_tables_summed_pl_kernel(
         w_dealt = keep.tile([P, N], I32, align_bytes=64)
         wd_dealt = keep.tile([P, N], I32, align_bytes=64)
         wscale_raw = keep.tile([P, N], U8)
-        wscale = keep.tile([P, N], U8, align_bytes=64)
         dx_codes = keep.tile([P, 2 * J], U8, align_bytes=64)
         dx_scale = keep.tile([P, J], U8, align_bytes=64)
         warm = keep.tile([P, 2], F32)
@@ -66,8 +64,8 @@ def tile_list_three_tables_summed_pl_kernel(
         def load_list(name):
             nc.sync.dma_start(lists[name][:], list_src[name])
 
-        def load_scales(tile, src, row, q):
-            nc.sync.dma_start(
+        def load_scales(eng, tile, src, row, q):
+            eng.dma_start(
                 tile[32 * q + row : 32 * q + row + 4, :].bitcast(I32),
                 src[0][4 * q : 4 * q + 4, :].bitcast(I32),
             )
@@ -77,23 +75,22 @@ def tile_list_three_tables_summed_pl_kernel(
 
         order = [("c", 0), ("c", 1), ("a", 0), ("a", 1), ("b", 0), ("c", 2),
                  ("b", 1), ("a", 2), ("c", 3), ("b", 2), ("a", 3), ("b", 3)]
-        small = [lambda: load_list("c"), lambda: load_list("a"), lambda: load_list("b"),
-                 lambda: nc.sync.dma_start(fk_sb[:], fk.rearrange("(p t) o -> p (t o)", t=PACK))]
         for q in range(4):
-            small.append(lambda q=q: load_scales(wscale_raw, wd_scales, 0, q))
+            load_scales(nc.gpsimd, wscale_raw, wd_scales, 0, q)
         for q in range(4):
-            small.append(lambda q=q: load_scales(wscale_raw, w_scales, W_ROW, q))
-        for q in range(4):
-            small.append(lambda q=q: load_scales(dx_scale, dx_scales, 0, q))
-        large = [lambda name=name, t=t: load_plane(name, t) for name, t in order]
-        large.insert(6, lambda: load_words(wd_raw, wd_words))
-        large.insert(8, lambda: load_words(w_raw, w_words))
-        large.insert(10, lambda: nc.sync.dma_start(dx_codes[:].bitcast(I32), dx_words[0].bitcast(I32)))
-        for i in range(len(large)):
-            large[i]()
-            small[i]()
-            if i == 5:
-                small[15]()
+            load_scales(nc.gpsimd, wscale_raw, w_scales, W_ROW, q)
+        for i, (name, t) in enumerate(order):
+            if (name, t) == ("a", 3):
+                load_words(wd_raw, wd_words)
+                nc.sync.dma_start(dx_codes[:].bitcast(I32), dx_words[0].bitcast(I32))
+            load_plane(name, t)
+            if i < 3:
+                load_list("cab"[i])
+            if 4 <= i < 8:
+                load_scales(nc.sync, dx_scale, dx_scales, 0, i - 4)
+            if i == 3:
+                nc.sync.dma_start(fk_sb[:], fk.rearrange("(p t) o -> p (t o)", t=PACK))
+        load_words(w_raw, w_words)
 
         s_bf = keep.tile([P, J, PACK], BF16, align_bytes=64)
         partial = {}
@@ -109,24 +106,22 @@ def tile_list_three_tables_summed_pl_kernel(
             nc.scalar.activation(s_bf[:, cols, t], src, COPY, scale=fk_sb[:, t : t + 1])
 
         whole = slice(0, J)
-        for name, t in order[:-2]:
-            dst = keep.tile([P, J], F32, name="sum_%s%d" % (name, t))
+        def deal(dst, src):
+            nc.vector.tensor_copy(
+                dst[:].rearrange("p (t m) -> p m t", t=PACK), src[:].rearrange("p (m t) -> p m t", t=PACK))
+
+        for name, t in order[:-1]:
+            if (name, t) == ("a", 3):
+                wscale = keep.tile([P, N], U8, tag="sum_a2", align_bytes=64)
+                nc.vector.tensor_copy(
+                    wscale[:].rearrange("p (t m) -> p t m", t=PACK),
+                    wscale_raw[:].rearrange("p (m t) -> p t m", t=PACK))
+                deal(wd_dealt, wd_raw)
+            dst = keep.tile([P, J], F32, name="sum_%s%d" % (name, t), tag="sum_%s%d" % (name, t), align_bytes=64)
             gather(name, t, whole, dst[:])
             partial[t, 0] = dst[:]
             if name == "b":
                 scale_round(t, whole, dst[:])
-            if (name, t) == ("b", 1):
-                nc.vector.tensor_copy(
-                    wd_dealt[:].rearrange("p (t m) -> p m t", t=PACK),
-                    wd_raw[:].rearrange("p (m t) -> p m t", t=PACK))
-            if (name, t) == ("a", 2):
-                nc.vector.tensor_copy(
-                    w_dealt[:].rearrange("p (t m) -> p m t", t=PACK),
-                    w_raw[:].rearrange("p (m t) -> p m t", t=PACK))
-            if (name, t) == ("b", 2):
-                nc.vector.tensor_copy(
-                    wscale[:].rearrange("p (t m) -> p t m", t=PACK),
-                    wscale_raw[:].rearrange("p (m t) -> p t m", t=PACK))
 
         banks = [psum.tile([P, PACK, W], F32, name="bank%d" % q) for q in range(PARTS)]
         for q in range(PARTS):
@@ -149,13 +144,13 @@ def tile_list_three_tables_summed_pl_kernel(
         out_words = out_1[0].rearrange("p c r -> p (c r)").bitcast(I32)
         for q in range(PARTS):
             cols = slice(q * W, (q + 1) * W)
-            two = ring.tile([P, W], F32, name="two")
-            partial[last, cols.start] = c_last[:, cols]
-            gather("a", last, cols, two[:])
             three = keep.tile([P, W], F32, name="three%d" % q)
-            partial[last, cols.start] = two[:]
+            partial[last, cols.start] = c_last[:, cols]
             gather("b", last, cols, three[:])
             scale_round(last, cols, three[:])
+        deal(w_dealt, w_raw)
+        for q in range(PARTS):
+            cols = slice(q * W, (q + 1) * W)
             nc.vector.quantize_mx(
                 s_codes[:, cols].bitcast(FP8X4), s_scale[:, cols],
                 s_bf[:, cols, :].rearrange("p j t -> p (j t)"))

from contextlib import ExitStack

import concourse.mybir as mybir

K, T, J, N = 512, 1024, 512, 512
FLOPS = 2 * 2 * K * N * J

F32 = mybir.dt.float32
BF16 = mybir.dt.bfloat16
I32 = mybir.dt.int32
U16 = mybir.dt.uint16
U8 = mybir.dt.uint8
FP8X4 = mybir.dt.float8_e4m3fn_x4
FP4X4 = mybir.dt.float4_e2m1fn_x4
ADD = mybir.AluOpType.add
COPY = mybir.ActivationFunctionType.Copy
SILU = mybir.ActivationFunctionType.Silu

P = 128
PACK = 4
PARTS = 4
W = J // PARTS
W_ROW = 4


def tile_list_three_tables_summed_pl_kernel(
    tc, xa, xb, xc, fk, w_words, w_scales, dx_words, dx_scales, wd_words, wd_scales,
    offs, offs2, offs3, out_0, out_1, out_2,
):
    nc = tc.nc
    with ExitStack() as ctx:
        keep = ctx.enter_context(tc.tile_pool(name="keep", bufs=1))
        psum = ctx.enter_context(tc.psum_pool(name="psum", bufs=1))

        lists = {}
        for name in ("c", "a", "b"):
            lists[name] = keep.tile([P, J // 16], U16, name="list_" + name)
        list_src = {"a": offs, "b": offs2, "c": offs3}
        table_src = {"a": xa, "b": xb, "c": xc}
        planes = {}
        for name in ("c", "a", "b"):
            for t in range(PACK):
                planes[name, t] = keep.tile([P, T], F32, name="plane_%s%d" % (name, t))

        fk_sb = keep.tile([P, PACK], F32)
        w_raw = keep.tile([P, N], I32)
        wd_raw = keep.tile([P, N], I32)
        w_dealt = keep.tile([P, N], I32, align_bytes=64)
        wd_dealt = keep.tile([P, N], I32, align_bytes=64)
        wscale_raw = keep.tile([P, N], U8)
        dx_codes = keep.tile([P, 2 * J], U8, align_bytes=64)
        dx_scale = keep.tile([P, J], U8, align_bytes=64)
        warm = keep.tile([P, 2], F32)

        nc.vector.memset(wscale_raw[:].bitcast(I32), 0)
        nc.vector.memset(dx_scale[:].bitcast(I32), 0)
        nc.vector.memset(warm[:, 0:1], 0.0)
        nc.scalar.activation(warm[:, 1:2], warm[:, 0:1], SILU)

        def load_plane(name, t):
            rows = table_src[name].rearrange("(p t) u -> p t u", t=PACK)
            nc.sync.dma_start(planes[name, t][:], rows[:, t, :])

        def load_list(name):
            nc.sync.dma_start(lists[name][:], list_src[name])

        def load_scales(eng, tile, src, row, q):
            eng.dma_start(
                tile[32 * q + row : 32 * q + row + 4, :].bitcast(I32),
                src[0][4 * q : 4 * q + 4, :].bitcast(I32),
            )

        def load_words(tile, src):
            nc.sync.dma_start(tile[:], src[0].rearrange("p n t -> p (n t)").bitcast(I32))

        order = [("c", 0), ("c", 1), ("a", 0), ("a", 1), ("b", 0), ("c", 2),
                 ("b", 1), ("a", 2), ("c", 3), ("b", 2), ("a", 3), ("b", 3)]
        for q in range(4):
            load_scales(nc.gpsimd, wscale_raw, wd_scales, 0, q)
        for q in range(4):
            load_scales(nc.gpsimd, wscale_raw, w_scales, W_ROW, q)
        for i, (name, t) in enumerate(order):
            if (name, t) == ("a", 3):
                load_words(wd_raw, wd_words)
                nc.sync.dma_start(dx_codes[:].bitcast(I32), dx_words[0].bitcast(I32))
            load_plane(name, t)
            if i < 3:
                load_list("cab"[i])
            if 4 <= i < 8:
                load_scales(nc.sync, dx_scale, dx_scales, 0, i - 4)
            if i == 3:
                nc.sync.dma_start(fk_sb[:], fk.rearrange("(p t) o -> p (t o)", t=PACK))
        load_words(w_raw, w_words)

        s_bf = keep.tile([P, J, PACK], BF16, align_bytes=64)
        partial = {}

        def gather(name, t, cols, into):
            picked = planes[name, t][:].indirect(lists[name][:, cols.start // 16 : cols.stop // 16])
            if name == "c":
                nc.vector.tensor_copy(into, picked)
            else:
                nc.vector.tensor_tensor(into, picked, partial[t, cols.start], ADD)

        def scale_round(t, cols, src):
            nc.scalar.activation(s_bf[:, cols, t], src, COPY, scale=fk_sb[:, t : t + 1])

        whole = slice(0, J)
        def deal(dst, src):
            nc.vector.tensor_copy(
                dst[:].rearrange("p (t m) -> p m t", t=PACK), src[:].rearrange("p (m t) -> p m t", t=PACK))

        for name, t in order[:-1]:
            if (name, t) == ("a", 3):
                wscale = keep.tile([P, N], U8, tag="sum_a2", align_bytes=64)
                nc.vector.tensor_copy(
                    wscale[:].rearrange("p (t m) -> p t m", t=PACK),
                    wscale_raw[:].rearrange("p (m t) -> p t m", t=PACK))
                deal(wd_dealt, wd_raw)
            dst = keep.tile([P, J], F32, name="sum_%s%d" % (name, t), tag="sum_%s%d" % (name, t), align_bytes=64)
            gather(name, t, whole, dst[:])
            partial[t, 0] = dst[:]
            if name == "b":
                scale_round(t, whole, dst[:])

        banks = [psum.tile([P, PACK, W], F32, name="bank%d" % q) for q in range(PARTS)]
        for q in range(PARTS):
            for t in range(PACK):
                nc.tensor.matmul_mx(
                    banks[q][:, t, :],
                    lhsT=wd_dealt[:, t * P : (t + 1) * P].bitcast(FP8X4),
                    lhsT_scale=wscale[:, t * P : (t + 1) * P],
                    rhs=dx_codes[:, 2 * q * W : 2 * (q + 1) * W].bitcast(FP4X4),
                    rhs_scale=dx_scale[:, q * W : (q + 1) * W],
                    start=(t == 0), stop=False)

        last = PACK - 1
        c_last = partial[last, 0]
        s_codes = keep.tile([P, J], I32, align_bytes=64)
        s_scale = keep.tile([P, J], U8, align_bytes=64)
        y_codes = keep.tile([P, J], I32, align_bytes=64)
        y_scale = keep.tile([P, J], U8, align_bytes=64)
        out_rows = out_0.rearrange("(p t) j -> p t j", t=PACK)
        out_words = out_1[0].rearrange("p c r -> p (c r)").bitcast(I32)
        for q in range(PARTS):
            cols = slice(q * W, (q + 1) * W)
            three = keep.tile([P, W], F32, name="three%d" % q)
            partial[last, cols.start] = c_last[:, cols]
            gather("b", last, cols, three[:])
            scale_round(last, cols, three[:])
        deal(w_dealt, w_raw)
        for q in range(PARTS):
            cols = slice(q * W, (q + 1) * W)
            nc.vector.quantize_mx(
                s_codes[:, cols].bitcast(FP8X4), s_scale[:, cols],
                s_bf[:, cols, :].rearrange("p j t -> p (j t)"))
            for t in range(PACK):
                nc.tensor.matmul_mx(
                    banks[q][:, t, :],
                    lhsT=w_dealt[:, t * P : (t + 1) * P].bitcast(FP8X4),
                    lhsT_scale=wscale[W_ROW:, t * P : (t + 1) * P],
                    rhs=s_codes[:, cols].bitcast(FP8X4),
                    rhs_scale=s_scale[:, cols],
                    start=False, stop=(t == last))
            y = keep.tile([P, PACK, W], F32, name="y%d" % q)
            nc.scalar.activation(y[:], banks[q][:], SILU, scale=0.6)
            nc.sync.dma_start(out_rows[:, :, cols], y[:])
            y_bf = keep.tile([P, W, PACK], BF16, name="y_bf%d" % q, align_bytes=64)
            nc.vector.tensor_copy(
                y_bf[:].rearrange("p (c i) t -> p c t i", i=4),
                y[:].rearrange("p t (c i) -> p c t i", i=4))
            nc.vector.quantize_mx(
                y_codes[:, cols].bitcast(FP8X4), y_scale[:, cols],
                y_bf[:].rearrange("p j t -> p (j t)"))
            nc.sync.dma_start(out_words[:, cols], y_codes[:, cols])
        for q in range(4):
            eng = nc.scalar if q % 2 else nc.sync
            eng.dma_start(
                out_2[0][4 * q : 4 * q + 4, :].bitcast(I32),
                y_scale[32 * q : 32 * q + 4, :].bitcast(I32))
